import numpy as np
import ml_dtypes


def mxq(x, axis, fmt="e4m3"):
    dtype, down = {"e4m3": (ml_dtypes.float8_e4m3fn, 7), "e5m2": (ml_dtypes.float8_e5m2, 14)}[fmt]
    v = np.moveaxis(np.asarray(x, np.float32).astype(ml_dtypes.bfloat16).astype(np.float64), axis, -1)
    blocks = v.reshape(v.shape[:-1] + (-1, 32))
    amax = np.abs(blocks).max(-1, keepdims=True)
    byte = np.maximum(np.where(amax > 0, np.frexp(amax)[1] - 1 + 127, 0) - down, 1)
    scale = np.exp2(byte - 127.0)
    codes = (blocks / scale).astype(np.float32).astype(dtype).astype(np.float64)
    return np.moveaxis((codes * scale).reshape(v.shape), -1, axis)


WIDE = False


def mx_kscale(k):
    if not WIDE:
        return np.ones(k)
    levels = np.array([10, -10, 5, -5, 0])
    if k % 512:
        return np.exp2(np.random.permutation(np.resize(levels, k // 32))).repeat(32)
    a = np.empty((k // 512, 16))
    for p in range(k // 512):
        a[p, :8] = np.random.permutation(np.resize(levels, 8))
        for g in range(8):
            far = levels[np.abs(levels - a[p, g]) >= 10]
            a[p, g + 8] = far[np.random.randint(len(far))]
    return np.exp2(a.ravel()).repeat(32)


def f64(x):
    return np.asarray(x).astype(np.float64)


def striped(idx):
    return np.tile(idx.reshape(-1, 16).T, (8, 1)).astype(np.uint16)


def unstriped(offs):
    return offs[:16].T.reshape(-1).astype(np.int64)


def pack_weight(w):
    k, n = w.shape
    w = f64(np.asarray(w, np.float32).astype(ml_dtypes.bfloat16)).reshape(k // 32, 32, n)
    amax = np.abs(w).max(1)
    byte = np.clip(np.where(amax > 0, np.frexp(amax)[1] - 1 + 127 - 7, 1), 1, 254)
    scaled = (w * np.exp2(127.0 - byte)[:, None, :]).reshape(k, n).astype(np.float32)
    words = np.ascontiguousarray(scaled.reshape(k // 512, 128, 4, n).transpose(0, 1, 3, 2)).astype(ml_dtypes.float8_e4m3fn).view(np.uint8)
    return words, np.ascontiguousarray(byte.astype(np.uint8).reshape(k // 512, 16, n))


def unpack_weight(words, scales):
    g, p, n, _ = words.shape
    vals = np.ascontiguousarray(words).view(ml_dtypes.float8_e4m3fn).astype(np.float64) * np.repeat(np.exp2(scales.astype(np.float64) - 127.0), 8, axis=1)[..., None]
    return vals.transpose(0, 1, 3, 2).reshape(g * 512, n)


def relu(v):
    return np.maximum(v, 0.0)


def sigmoid(v):
    return 1.0 / (1.0 + np.exp(-np.maximum(v, -700.0)))


K, T, S, D, H, Z, W = 512, 2048, 512, 2, 512, 512, 2048
P = 2 ** 7


def setup_inputs():
    n = np.random.standard_normal
    s = mx_kscale(K)[:, None]
    u = mx_kscale(H)
    packed_xT = pack_weight(n((K, T)) * s)
    packed_eT = pack_weight(n((K, W)) * s)
    return {
        "x_words": packed_xT[0],
        "x_scales": packed_xT[1],
        "w1": (n((K, H)) / np.sqrt(K) / s).astype(np.float32),
        "e_words": packed_eT[0],
        "e_scales": packed_eT[1],
        "w2": (n((K, H)) / np.sqrt(K) / s).astype(np.float32),
        "w3": (n((K, H)) / np.sqrt(K) / s).astype(np.float32),
        "unit": (np.random.uniform(0.6, 1.4, (H, 1)) * u[:, None]).astype(np.float32),
        "unit2": (np.random.uniform(0.6, 1.4, (H, 1)) / np.sqrt(H) / u[:, None]).astype(np.float32),
        "imm": (np.tile(np.random.uniform(0.3, 1.2, W), (P, 1))).astype(np.float32),
        "offs": striped(np.random.permutation(T)[:S]),
        "agn": striped(np.random.permutation(W)[:Z]),
        "mut": striped(np.random.permutation(Z)),
        "esc": striped(np.random.permutation(Z)),
    }


def reference(x_words, x_scales, w1, e_words, e_scales, w2, w3, unit, unit2, imm, offs, agn, mut, esc):
    xq = unpack_weight(x_words, x_scales)[:, unstriped(offs)]
    y = mxq(f64(w1), 0, "e4m3").T @ xq
    absy = np.abs(y)
    par_ = (y.reshape(len(y), -1, D).sum(axis=2)) / (absy.reshape(len(absy), -1, D).max(axis=2) + 0.5)
    hid = f64(unit) * par_
    e_agn = unpack_weight(e_words, e_scales)[:, unstriped(agn)]
    ye = mxq(f64(w2), 0, "e4m3").T @ e_agn
    yw = mxq(f64(w3), 0, "e4m3").T @ e_agn
    wm = yw[:, unstriped(mut)]
    epi = ye - (0.8 * relu(wm))
    hid2 = f64(unit2) * epi
    sc = mxq(hid, 0, "e4m3").T @ mxq(hid2, 0, "e4m3")
    bind = sigmoid(2.0 * sc)
    be = bind[:, unstriped(esc)]
    return (bind * (-1.0 * (0.7 * be) + 1.0)) * (f64(imm)[:1][:, unstriped(agn)])

@@ -1,0 +1,265 @@
+from contextlib import ExitStack
+
+import concourse.mybir as mybir
+
+F32 = mybir.dt.float32
+BF16 = mybir.dt.bfloat16
+I32 = mybir.dt.int32
+U32 = mybir.dt.uint32
+U16 = mybir.dt.uint16
+U8 = mybir.dt.uint8
+FP8X4 = mybir.dt.float8_e4m3fn_x4
+ALU = mybir.AluOpType
+ACT = mybir.ActivationFunctionType
+
+P = 128
+PACK = 4
+TABLE = 2048
+PICKED = 512
+PAIRS = 256
+HALF = 256
+
+FLOPS = 2 * 512 * 512 * 512 * 3 + 2 * 512 * 256 * 512
+BYTES = 5 * 1048576 + 2 * 32768 + 2 * 2048 + 8192 + 4 * 8192 + 256 * 512 * 4
+
+
+def tile_picked_yglycan_esc_p_kernel(
+    tc, x_words, x_scales, w1, e_words, e_scales, w2, w3, unit, unit2, imm, offs, agn, mut, esc, out
+):
+    nc = tc.nc
+    with ExitStack() as ctx:
+        keep = ctx.enter_context(tc.tile_pool(name="keep", bufs=1))
+        psum = ctx.enter_context(tc.psum_pool(name="psum", bufs=1))
+
+        def sb(name, shape, dtype):
+            return keep.tile(shape, dtype, name=name, align_bytes=64)
+
+        def load_list(name, src):
+            t = sb(name, [P, PICKED // 16], U16)
+            nc.sync.dma_start(t[:], src)
+            return t
+
+        def load_scales(name, src, queue):
+            t = sb(name, [P, TABLE], U8)
+            for q in range(4):
+                rows = src[0, 4 * q : 4 * q + 4, :].bitcast(I32)
+                queue.dma_start(t[32 * q : 32 * q + 32, :].bitcast(I32), rows.unsqueeze(0).broadcast_to([8, 4, TABLE // 4]))
+            return t
+
+        def load_words(name, src):
+            t = sb(name, [P, TABLE], U32)
+            nc.sync.dma_start(t[:].bitcast(I32), src[0].rearrange("p n t -> p (n t)").bitcast(I32))
+            return t
+
+        def load_weight(name, w):
+            halves = []
+            for h in range(2):
+                raw = sb(name + "_raw%d" % h, [P, PACK, HALF], F32)
+                nc.sync.dma_start(raw[:], w.rearrange("(p j) c -> p j c", j=PACK)[:, :, h * HALF : (h + 1) * HALF])
+                halves.append(raw)
+            return halves
+
+        def weight_half(name, w, h):
+            raw = sb(name + "_raw%d" % h, [P, PACK, HALF], F32)
+            nc.sync.dma_start(raw[:], w.rearrange("(p j) c -> p j c", j=PACK)[:, :, h * HALF : (h + 1) * HALF])
+            return raw
+
+        es_tab = sb("es_tab", [P, TABLE], U8)
+        nc.vector.memset(es_tab[:].bitcast(I32), 0)
+        offs_t = load_list("offs_t", offs)
+        xs_tab = load_scales("xs_tab", x_scales, nc.sync)
+        agn_t = load_list("agn_t", agn)
+        xw_tab = load_words("xw_tab", x_words)
+        w1_raw = [weight_half("w1", w1, 0)]
+        for q in range(4):
+            nc.sync.dma_start(es_tab[32 * q : 32 * q + 4, :].bitcast(I32), e_scales[0, 4 * q : 4 * q + 4, :].bitcast(I32))
+        w1_raw.append(weight_half("w1", w1, 1))
+        ew_tab = load_words("ew_tab", e_words)
+        w3_raw = load_weight("w3", w3)
+        w2_raw = load_weight("w2", w2)
+        mut_t = load_list("mut_t", mut)
+        esc_t = load_list("esc_t", esc)
+        imm_tab = sb("imm_tab", [P, TABLE], F32)
+        nc.sync.dma_start(imm_tab[:], imm)
+
+        u1 = sb("u1", [P, PACK], F32)
+        u2 = sb("u2", [P, PACK], F32)
+        nc.gpsimd.dma_start(u1[:], unit.rearrange("(p t) o -> p (t o)", t=PACK))
+        nc.gpsimd.dma_start(u2[:], unit2.rearrange("(p t) o -> p (t o)", t=PACK))
+        step = sb("step", [P, PACK], F32)
+        flip = sb("flip", [P, PACK], F32)
+        u1f = sb("u1f", [P, PACK], F32)
+        u2f = sb("u2f", [P, PACK], F32)
+        zsc = sb("zsc", [P, PACK], F32)
+        nc.gpsimd.tensor_scalar(step[:], u2[:], 0.0, -2.0, ALU.is_ge, ALU.mult)
+        nc.gpsimd.tensor_scalar(flip[:], step[:], 1.0, 1.0, ALU.mult, ALU.add)
+        nc.gpsimd.tensor_tensor(u1f[:], u1[:], flip[:], ALU.mult)
+        nc.gpsimd.tensor_tensor(u2f[:], u2[:], flip[:], ALU.mult)
+        nc.gpsimd.tensor_scalar(zsc[:], u2f[:], -0.8, 0.0, ALU.mult, ALU.add)
+
+        def gather(name, table, offsets, dtype):
+            t = sb(name, [P, PICKED], dtype)
+            nc.vector.tensor_copy(t[:], table[:].indirect(offsets[:]))
+            return t
+
+        def gp_cast(dst, src):
+            nc.gpsimd.tensor_scalar(dst, src, 1.0, 0.0, ALU.mult, ALU.add)
+
+        def cast(copy, grouped, raw, h):
+            dealt = grouped[:].rearrange("p (t m j) -> p m t j ", t=PACK, j=PACK)
+            copy(dealt[:, h * 64 : (h + 1) * 64], raw[h][:].rearrange("p j (m t) -> p m t j", t=PACK))
+
+        def quantise(grouped, codes, scales, calls):
+            width = PACK * P // calls
+            for c in range(calls):
+                cols = slice(c * width, (c + 1) * width)
+                nc.vector.quantize_mx(codes[:, cols].bitcast(FP8X4), scales[:, cols], grouped[:, c * width * PACK : (c + 1) * width * PACK])
+
+        def product(tag, codes, scales, t, words, bytes_):
+            bank = psum.tile([P, PICKED], F32, name=tag, tag=tag)
+            cols = slice(t * P, (t + 1) * P)
+            nc.tensor.matmul_mx(
+                bank[:], lhsT=codes[:, cols].bitcast(FP8X4), lhsT_scale=scales[:, cols],
+                rhs=words[:].bitcast(FP8X4), rhs_scale=bytes_[:], start=True, stop=True,
+            )
+            return bank
+
+        def woven(tile):
+            return tile[:].rearrange("p (c i t) -> p c t i", i=4, t=PACK)
+
+        def planes(tile):
+            return tile[:].rearrange("p t (c i) -> p c t i", i=4)
+
+        w1_bf, w2_bf, w3_bf = [sb("w%d_bf" % w, [P, PACK * P * PACK], BF16) for w in (1, 2, 3)]
+        w1_c, w2_c, w3_c = [sb("w%d_c" % w, [P, PACK * P], U32) for w in (1, 2, 3)]
+        w1_s, w2_s, w3_s = [sb("w%d_s" % w, [P, PACK * P], U8) for w in (1, 2, 3)]
+        big = sb("big", [P, PACK, PAIRS], F32)
+        su = sb("su", [P, PACK, PAIRS], F32)
+        logd = sb("logd", [P, PACK, PAIRS], F32)
+        recip = sb("recip", [P, PACK, PAIRS], F32)
+        immg = sb("immg", [P, PICKED], F32)
+        hid = sb("hid", [P, PAIRS * PACK], BF16)
+        hc = sb("hc", [P, PAIRS], U32)
+        hs = sb("hs", [P, PAIRS], U8)
+        z = [sb("z%d" % t, [P, PICKED], F32) for t in range(PACK)]
+        yes = [sb("yes%d" % t, [P, PICKED], F32) for t in range(PACK)]
+        ye = [None] * PACK
+        epi = [sb("epi%d" % h, [P, PACK, HALF], F32) for h in range(2)]
+        hid2 = [sb("hid2_%d" % h, [P, HALF * PACK], BF16) for h in range(2)]
+        h2c = [sb("h2c%d" % h, [P, HALF], U32) for h in range(2)]
+        h2s = [sb("h2s%d" % h, [P, HALF], U8) for h in range(2)]
+        th = [sb("th%d" % b, [P, PICKED], F32) for b in range(2)]
+        pre = [sb("pre%d" % b, [P, PICKED], F32) for b in range(2)]
+        shifted = sb("shifted", [P, PICKED], F32)
+
+        def paratope(t):
+            y = product("a%d" % t, w1_c, w1_s, t, xw, xs)
+            pair = y[:].rearrange("p (v d) -> p d v", d=2)
+            absy = sb("absy%d" % t, [P, 2, PAIRS], F32)
+            odd = sb("odd%d" % t, [P, PAIRS], F32)
+            nc.scalar.activation(absy[:], pair, ACT.Abs)
+            nc.scalar.activation(odd[:], pair[:, 1, :], ACT.Copy, scale=u1f[:, t : t + 1])
+            nc.vector.tensor_tensor(big[:, t, :], absy[:, 0, :], absy[:, 1, :], ALU.max)
+            nc.vector.scalar_tensor_tensor(su[:, t, :], pair[:, 0, :], u1f[:, t : t + 1], odd[:], ALU.mult, ALU.add)
+
+        def rectify(t):
+            yw = product("b%d" % t, w3_c, w3_s, t, ew, es)
+            nc.scalar.activation(z[t][:], yw[:], ACT.Relu, scale=zsc[:, t : t + 1])
+
+        def half(h):
+            return slice(h * HALF, (h + 1) * HALF)
+
+        def picks(lst, h):
+            return lst[:, h * 16 : (h + 1) * 16]
+
+        def fetch(t, h):
+            nc.scalar.activation(yes[t][:, half(h)], z[t][:].indirect(picks(mut_t, h)), ACT.Copy)
+
+        def join(t, h):
+            nc.vector.scalar_tensor_tensor(epi[h][:, t, :], ye[t][:, half(h)], u2f[:, t : t + 1], yes[t][:, half(h)], ALU.mult, ALU.add)
+
+        def fetch_join(t, h):
+            nc.vector.tensor_tensor(epi[h][:, t, :], z[t][:].indirect(picks(mut_t, h)), yes[t][:, half(h)], ALU.add)
+
+        def bind(h, b):
+            tag = "b%d" % (2 * h + b)
+            sc = psum.tile([P, HALF], F32, name=tag, tag=tag)
+            rows = slice(b * P, (b + 1) * P)
+            nc.tensor.matmul_mx(
+                sc[:], lhsT=hc[:, rows].bitcast(FP8X4), lhsT_scale=hs[:, rows],
+                rhs=h2c[h][:].bitcast(FP8X4), rhs_scale=h2s[h][:], start=True, stop=True,
+            )
+            nc.scalar.activation(th[b][:, half(h)], sc[:], ACT.Tanh)
+            if b == 0:
+                nc.scalar.activation(shifted[:, half(h)], th[0][:, half(h)], ACT.Copy, bias=-0.65 / 0.35)
+            nc.vector.scalar_tensor_tensor(pre[b][:, half(h)], th[b][:, half(h)], 1.0, immg[:, half(h)], ALU.add, ALU.mult)
+
+        def escape_fused(h):
+            res = sb("res0_%d" % h, [P, HALF], F32)
+            nc.vector.tensor_tensor(res[:], shifted[:].indirect(picks(esc_t, h)), pre[0][:, half(h)], ALU.mult)
+            nc.sync.dma_start(out[0:P, half(h)], res[:])
+
+        def escape_split(h):
+            got = sb("got%d" % h, [P, HALF], F32)
+            nc.scalar.activation(got[:], th[1][:].indirect(picks(esc_t, h)), ACT.Copy)
+            res = sb("res1_%d" % h, [P, HALF], F32)
+            nc.vector.scalar_tensor_tensor(res[:], got[:], -0.65 / 0.35, pre[1][:, half(h)], ALU.add, ALU.mult)
+            nc.sync.dma_start(out[P : 2 * P, half(h)], res[:])
+
+        xs = gather("xs", xs_tab, offs_t, U8)
+        xw = gather("xw", xw_tab, offs_t, U32)
+        es = gather("es", es_tab, agn_t, U8)
+        cast(nc.scalar.copy, w1_bf, w1_raw, 0)
+        cast(nc.vector.tensor_copy, w1_bf, w1_raw, 1)
+        quantise(w1_bf, w1_c, w1_s, 4)
+        paratope(0)
+        paratope(1)
+        paratope(2)
+        paratope(3)
+        ew = gather("ew", ew_tab, agn_t, U32)
+        cast(nc.vector.tensor_copy, w3_bf, w3_raw, 0)
+        cast(nc.vector.tensor_copy, w3_bf, w3_raw, 1)
+        quantise(w3_bf, w3_c, w3_s, 2)
+        nc.scalar.activation(logd[:, 0:2, :], big[:, 0:2, :], ACT.Ln, bias=0.5)
+        nc.scalar.activation(logd[:, 2:4, :], big[:, 2:4, :], ACT.Ln, bias=0.5)
+        rectify(0)
+        rectify(1)
+        rectify(2)
+        rectify(3)
+        cast(nc.vector.tensor_copy, w2_bf, w2_raw, 0)
+        cast(nc.vector.tensor_copy, w2_bf, w2_raw, 1)
+        quantise(w2_bf, w2_c, w2_s, 2)
+        ye[0] = product("a0", w2_c, w2_s, 0, ew, es)
+        nc.scalar.activation(yes[0][:], ye[0][:], ACT.Copy, scale=u2f[:, 0 : 1])
+        ye[1] = product("a1", w2_c, w2_s, 1, ew, es)
+        nc.scalar.activation(yes[1][:], ye[1][:], ACT.Copy, scale=u2f[:, 1 : 2])
+        ye[2] = product("a2", w2_c, w2_s, 2, ew, es)
+        ye[3] = product("a3", w2_c, w2_s, 3, ew, es)
+        fetch(2, 0)
+        fetch(3, 0)
+        fetch(2, 1)
+        fetch(3, 1)
+        nc.scalar.activation(recip[:], logd[:], ACT.Exp, scale=-1.0)
+        nc.scalar.activation(immg[:], imm_tab[:].indirect(agn_t[:]), ACT.Copy, scale=-0.175)
+        fetch_join(0, 0)
+        fetch_join(1, 0)
+        join(2, 0)
+        join(3, 0)
+        nc.vector.tensor_copy(woven(hid2[0]), planes(epi[0]))
+        nc.vector.tensor_tensor(woven(hid), planes(su), planes(recip), ALU.mult)
+        nc.vector.quantize_mx(h2c[0][:].bitcast(FP8X4), h2s[0][:], hid2[0][:])
+        nc.vector.quantize_mx(hc[:].bitcast(FP8X4), hs[:], hid[:])
+        fetch_join(0, 1)
+        fetch_join(1, 1)
+        join(2, 1)
+        join(3, 1)
+        nc.vector.tensor_copy(woven(hid2[1]), planes(epi[1]))
+        nc.vector.quantize_mx(h2c[1][:].bitcast(FP8X4), h2s[1][:], hid2[1][:])
+        bind(0, 0)
+        bind(0, 1)
+        bind(1, 0)
+        bind(1, 1)
+        escape_fused(0)
+        escape_split(0)
+        escape_fused(1)
+        escape_split(1)

@@ -31,20 +31,17 @@ def tile_picked_yglycan_esc_p_kernel(
         keep = ctx.enter_context(tc.tile_pool(name="keep", bufs=1))
         psum = ctx.enter_context(tc.psum_pool(name="psum", bufs=1))
 
-        def sb(name, shape, dtype):
-            return keep.tile(shape, dtype, name=name, align_bytes=64)
+        def sb(name, shape, dtype, tag=None):
+            return keep.tile(shape, dtype, name=name, tag=tag or name, align_bytes=64)
 
         def load_list(name, src):
             t = sb(name, [P, PICKED // 16], U16)
             nc.sync.dma_start(t[:], src)
             return t
 
-        def load_scales(name, src, queue):
-            t = sb(name, [P, TABLE], U8)
+        def load_scales(table, src):
             for q in range(4):
-                rows = src[0, 4 * q : 4 * q + 4, :].bitcast(I32)
-                queue.dma_start(t[32 * q : 32 * q + 32, :].bitcast(I32), rows.unsqueeze(0).broadcast_to([8, 4, TABLE // 4]))
-            return t
+                nc.sync.dma_start(table[32 * q : 32 * q + 4, :].bitcast(I32), src[0, 4 * q : 4 * q + 4, :].bitcast(I32))
 
         def load_words(name, src):
             t = sb(name, [P, TABLE], U32)
@@ -52,50 +49,35 @@ def tile_picked_yglycan_esc_p_kernel(
             return t
 
         def load_weight(name, w):
-            halves = []
-            for h in range(2):
-                raw = sb(name + "_raw%d" % h, [P, PACK, HALF], F32)
-                nc.sync.dma_start(raw[:], w.rearrange("(p j) c -> p j c", j=PACK)[:, :, h * HALF : (h + 1) * HALF])
-                halves.append(raw)
-            return halves
-
-        def weight_half(name, w, h):
-            raw = sb(name + "_raw%d" % h, [P, PACK, HALF], F32)
-            nc.sync.dma_start(raw[:], w.rearrange("(p j) c -> p j c", j=PACK)[:, :, h * HALF : (h + 1) * HALF])
+            raw = sb(name + "_raw", [P, PACK, PACK * P], F32)
+            nc.sync.dma_start(raw[:], w.rearrange("(p j) c -> p j c", j=PACK))
             return raw
 
+        xs_tab = sb("xs_tab", [P, TABLE], U8)
+        nc.gpsimd.memset(xs_tab[:].bitcast(I32), 0)
         es_tab = sb("es_tab", [P, TABLE], U8)
         nc.vector.memset(es_tab[:].bitcast(I32), 0)
+        imm_tab = sb("imm_tab", [P, TABLE], F32)
         offs_t = load_list("offs_t", offs)
-        xs_tab = load_scales("xs_tab", x_scales, nc.sync)
         agn_t = load_list("agn_t", agn)
+        load_scales(xs_tab, x_scales)
+        warm = sb("warm", [P, 1], F32)
+        nc.gpsimd.memset(warm[:], 1.0)
+        warm2 = sb("warm2", [P, 1], F32)
+        nc.scalar.activation(warm2[:], warm[:], ACT.Ln)
+        u1 = sb("u1", [P, PACK], F32)
+        u2 = sb("u2", [P, PACK], F32)
+        nc.gpsimd.dma_start(u2[:], unit2.rearrange("(p t) o -> p (t o)", t=PACK))
+        nc.gpsimd.dma_start(u1[:], unit.rearrange("(p t) o -> p (t o)", t=PACK))
+        w1_raw = load_weight("w1", w1)
+        load_scales(es_tab, e_scales)
         xw_tab = load_words("xw_tab", x_words)
-        w1_raw = [weight_half("w1", w1, 0)]
-        for q in range(4):
-            nc.sync.dma_start(es_tab[32 * q : 32 * q + 4, :].bitcast(I32), e_scales[0, 4 * q : 4 * q + 4, :].bitcast(I32))
-        w1_raw.append(weight_half("w1", w1, 1))
-        ew_tab = load_words("ew_tab", e_words)
         w3_raw = load_weight("w3", w3)
+        ew_tab = load_words("ew_tab", e_words)
         w2_raw = load_weight("w2", w2)
         mut_t = load_list("mut_t", mut)
         esc_t = load_list("esc_t", esc)
-        imm_tab = sb("imm_tab", [P, TABLE], F32)
         nc.sync.dma_start(imm_tab[:], imm)
-
-        u1 = sb("u1", [P, PACK], F32)
-        u2 = sb("u2", [P, PACK], F32)
-        nc.gpsimd.dma_start(u1[:], unit.rearrange("(p t) o -> p (t o)", t=PACK))
-        nc.gpsimd.dma_start(u2[:], unit2.rearrange("(p t) o -> p (t o)", t=PACK))
-        step = sb("step", [P, PACK], F32)
-        flip = sb("flip", [P, PACK], F32)
-        u1f = sb("u1f", [P, PACK], F32)
-        u2f = sb("u2f", [P, PACK], F32)
-        zsc = sb("zsc", [P, PACK], F32)
-        nc.gpsimd.tensor_scalar(step[:], u2[:], 0.0, -2.0, ALU.is_ge, ALU.mult)
-        nc.gpsimd.tensor_scalar(flip[:], step[:], 1.0, 1.0, ALU.mult, ALU.add)
-        nc.gpsimd.tensor_tensor(u1f[:], u1[:], flip[:], ALU.mult)
-        nc.gpsimd.tensor_tensor(u2f[:], u2[:], flip[:], ALU.mult)
-        nc.gpsimd.tensor_scalar(zsc[:], u2f[:], -0.8, 0.0, ALU.mult, ALU.add)
 
         def gather(name, table, offsets, dtype):
             t = sb(name, [P, PICKED], dtype)
@@ -105,9 +87,9 @@ def tile_picked_yglycan_esc_p_kernel(
         def gp_cast(dst, src):
             nc.gpsimd.tensor_scalar(dst, src, 1.0, 0.0, ALU.mult, ALU.add)
 
-        def cast(copy, grouped, raw, h):
-            dealt = grouped[:].rearrange("p (t m j) -> p m t j ", t=PACK, j=PACK)
-            copy(dealt[:, h * 64 : (h + 1) * 64], raw[h][:].rearrange("p j (m t) -> p m t j", t=PACK))
+        def cast(copy, grouped, raw, m0, m1):
+            dealt = grouped[:].rearrange("p (t m j) -> p m t j", t=PACK, j=PACK)
+            copy(dealt[:, m0:m1], raw[:].rearrange("p j (m t) -> p m t j", t=PACK)[:, m0:m1])
 
         def quantise(grouped, codes, scales, calls):
             width = PACK * P // calls
@@ -133,8 +115,6 @@ def tile_picked_yglycan_esc_p_kernel(
         w1_bf, w2_bf, w3_bf = [sb("w%d_bf" % w, [P, PACK * P * PACK], BF16) for w in (1, 2, 3)]
         w1_c, w2_c, w3_c = [sb("w%d_c" % w, [P, PACK * P], U32) for w in (1, 2, 3)]
         w1_s, w2_s, w3_s = [sb("w%d_s" % w, [P, PACK * P], U8) for w in (1, 2, 3)]
-        big = sb("big", [P, PACK, PAIRS], F32)
-        su = sb("su", [P, PACK, PAIRS], F32)
         logd = sb("logd", [P, PACK, PAIRS], F32)
         recip = sb("recip", [P, PACK, PAIRS], F32)
         immg = sb("immg", [P, PICKED], F32)
@@ -207,27 +187,36 @@ def tile_picked_yglycan_esc_p_kernel(
             nc.sync.dma_start(out[P : 2 * P, half(h)], res[:])
 
         xs = gather("xs", xs_tab, offs_t, U8)
-        xw = gather("xw", xw_tab, offs_t, U32)
-        es = gather("es", es_tab, agn_t, U8)
-        cast(nc.scalar.copy, w1_bf, w1_raw, 0)
-        cast(nc.vector.tensor_copy, w1_bf, w1_raw, 1)
+        cast(nc.scalar.copy, w1_bf, w1_raw, 0, 48)
+        cast(nc.vector.tensor_copy, w1_bf, w1_raw, 48, 128)
+        factors = sb("factors", [P, 4, PACK], F32, tag="w1_raw")
+        flip, zsc, u2f, u1f = [factors[:, i, :] for i in range(4)]
+        nc.scalar.activation(flip[:], u2[:], ACT.Sign, scale=-1.0)
+        nc.scalar.activation(zsc[:], u2[:], ACT.Abs, scale=0.8)
+        nc.scalar.activation(u2f[:], zsc[:], ACT.Copy, scale=-1.25)
+        for t in range(PACK):
+            nc.scalar.activation(u1f[:, t : t + 1], u1[:, t : t + 1], ACT.Copy, scale=flip[:, t : t + 1])
         quantise(w1_bf, w1_c, w1_s, 4)
+        es = gather("es", es_tab, agn_t, U8)
+        xw = gather("xw", xw_tab, offs_t, U32)
+        cast(nc.vector.tensor_copy, w3_bf, w3_raw, 0, 64)
+        cast(nc.vector.tensor_copy, w3_bf, w3_raw, 64, 128)
+        pooled = sb("pooled", [P, 2, PACK, PAIRS], F32, tag="w3_raw")
+        big, su = pooled[:, 0], pooled[:, 1]
         paratope(0)
         paratope(1)
         paratope(2)
         paratope(3)
-        ew = gather("ew", ew_tab, agn_t, U32)
-        cast(nc.vector.tensor_copy, w3_bf, w3_raw, 0)
-        cast(nc.vector.tensor_copy, w3_bf, w3_raw, 1)
         quantise(w3_bf, w3_c, w3_s, 2)
+        ew = gather("ew", ew_tab, agn_t, U32)
         nc.scalar.activation(logd[:, 0:2, :], big[:, 0:2, :], ACT.Ln, bias=0.5)
         nc.scalar.activation(logd[:, 2:4, :], big[:, 2:4, :], ACT.Ln, bias=0.5)
         rectify(0)
         rectify(1)
         rectify(2)
         rectify(3)
-        cast(nc.vector.tensor_copy, w2_bf, w2_raw, 0)
-        cast(nc.vector.tensor_copy, w2_bf, w2_raw, 1)
+        cast(nc.vector.tensor_copy, w2_bf, w2_raw, 0, 64)
+        cast(nc.vector.tensor_copy, w2_bf, w2_raw, 64, 128)
         quantise(w2_bf, w2_c, w2_s, 2)
         ye[0] = product("a0", w2_c, w2_s, 0, ew, es)
         nc.scalar.activation(yes[0][:], ye[0][:], ACT.Copy, scale=u2f[:, 0 : 1])
@@ -241,14 +230,14 @@ def tile_picked_yglycan_esc_p_kernel(
         fetch(3, 1)
         nc.scalar.activation(recip[:], logd[:], ACT.Exp, scale=-1.0)
         nc.scalar.activation(immg[:], imm_tab[:].indirect(agn_t[:]), ACT.Copy, scale=-0.175)
+        nc.vector.tensor_tensor(woven(hid), planes(su), planes(recip), ALU.mult)
+        nc.vector.quantize_mx(hc[:].bitcast(FP8X4), hs[:], hid[:])
         fetch_join(0, 0)
         fetch_join(1, 0)
         join(2, 0)
         join(3, 0)
-        nc.vector.tensor_copy(woven(hid2[0]), planes(epi[0]))
-        nc.vector.tensor_tensor(woven(hid), planes(su), planes(recip), ALU.mult)
+        nc.scalar.copy(woven(hid2[0]), planes(epi[0]))
         nc.vector.quantize_mx(h2c[0][:].bitcast(FP8X4), h2s[0][:], hid2[0][:])
-        nc.vector.quantize_mx(hc[:].bitcast(FP8X4), hs[:], hid[:])
         fetch_join(0, 1)
         fetch_join(1, 1)
         join(2, 1)

@@ -58,8 +58,8 @@ def tile_picked_yglycan_esc_p_kernel(
         es_tab = sb("es_tab", [P, TABLE], U8)
         nc.vector.memset(es_tab[:].bitcast(I32), 0)
         imm_tab = sb("imm_tab", [P, TABLE], F32)
+        w1_raw = load_weight("w1", w1)
         offs_t = load_list("offs_t", offs)
-        agn_t = load_list("agn_t", agn)
         load_scales(xs_tab, x_scales)
         warm = sb("warm", [P, 1], F32)
         nc.gpsimd.memset(warm[:], 1.0)
@@ -69,9 +69,9 @@ def tile_picked_yglycan_esc_p_kernel(
         u2 = sb("u2", [P, PACK], F32)
         nc.gpsimd.dma_start(u2[:], unit2.rearrange("(p t) o -> p (t o)", t=PACK))
         nc.gpsimd.dma_start(u1[:], unit.rearrange("(p t) o -> p (t o)", t=PACK))
-        w1_raw = load_weight("w1", w1)
-        load_scales(es_tab, e_scales)
         xw_tab = load_words("xw_tab", x_words)
+        agn_t = load_list("agn_t", agn)
+        load_scales(es_tab, e_scales)
         w3_raw = load_weight("w3", w3)
         ew_tab = load_words("ew_tab", e_words)
         w2_raw = load_weight("w2", w2)
@@ -170,8 +170,6 @@ def tile_picked_yglycan_esc_p_kernel(
                 rhs=h2c[h][:].bitcast(FP8X4), rhs_scale=h2s[h][:], start=True, stop=True,
             )
             nc.scalar.activation(th[b][:, half(h)], sc[:], ACT.Tanh)
-            if b == 0:
-                nc.scalar.activation(shifted[:, half(h)], th[0][:, half(h)], ACT.Copy, bias=-0.65 / 0.35)
             nc.vector.scalar_tensor_tensor(pre[b][:, half(h)], th[b][:, half(h)], 1.0, immg[:, half(h)], ALU.add, ALU.mult)
 
         def escape_fused(h):
@@ -186,7 +184,6 @@ def tile_picked_yglycan_esc_p_kernel(
             nc.vector.scalar_tensor_tensor(res[:], got[:], -0.65 / 0.35, pre[1][:, half(h)], ALU.add, ALU.mult)
             nc.sync.dma_start(out[P : 2 * P, half(h)], res[:])
 
-        xs = gather("xs", xs_tab, offs_t, U8)
         cast(nc.scalar.copy, w1_bf, w1_raw, 0, 48)
         cast(nc.vector.tensor_copy, w1_bf, w1_raw, 48, 128)
         factors = sb("factors", [P, 4, PACK], F32, tag="w1_raw")
@@ -197,8 +194,9 @@ def tile_picked_yglycan_esc_p_kernel(
         for t in range(PACK):
             nc.scalar.activation(u1f[:, t : t + 1], u1[:, t : t + 1], ACT.Copy, scale=flip[:, t : t + 1])
         quantise(w1_bf, w1_c, w1_s, 4)
-        es = gather("es", es_tab, agn_t, U8)
+        xs = gather("xs", xs_tab, offs_t, U8)
         xw = gather("xw", xw_tab, offs_t, U32)
+        es = gather("es", es_tab, agn_t, U8)
         cast(nc.vector.tensor_copy, w3_bf, w3_raw, 0, 64)
         cast(nc.vector.tensor_copy, w3_bf, w3_raw, 64, 128)
         pooled = sb("pooled", [P, 2, PACK, PAIRS], F32, tag="w3_raw")
@@ -245,10 +243,11 @@ def tile_picked_yglycan_esc_p_kernel(
         nc.vector.tensor_copy(woven(hid2[1]), planes(epi[1]))
         nc.vector.quantize_mx(h2c[1][:].bitcast(FP8X4), h2s[1][:], hid2[1][:])
         bind(0, 0)
-        bind(0, 1)
         bind(1, 0)
+        nc.scalar.activation(shifted[:], th[0][:], ACT.Copy, bias=-0.65 / 0.35)
+        bind(0, 1)
         bind(1, 1)
         escape_fused(0)
-        escape_split(0)
         escape_fused(1)
+        escape_split(0)
         escape_split(1)

from contextlib import ExitStack

import concourse.mybir as mybir

F32 = mybir.dt.float32
BF16 = mybir.dt.bfloat16
I32 = mybir.dt.int32
U32 = mybir.dt.uint32
U16 = mybir.dt.uint16
U8 = mybir.dt.uint8
FP8X4 = mybir.dt.float8_e4m3fn_x4
ALU = mybir.AluOpType
ACT = mybir.ActivationFunctionType

P = 128
PACK = 4
TABLE = 2048
PICKED = 512
PAIRS = 256
HALF = 256

FLOPS = 2 * 512 * 512 * 512 * 3 + 2 * 512 * 256 * 512
BYTES = 5 * 1048576 + 2 * 32768 + 2 * 2048 + 8192 + 4 * 8192 + 256 * 512 * 4


def tile_picked_yglycan_esc_p_kernel(
    tc, x_words, x_scales, w1, e_words, e_scales, w2, w3, unit, unit2, imm, offs, agn, mut, esc, out
):
    nc = tc.nc
    with ExitStack() as ctx:
        keep = ctx.enter_context(tc.tile_pool(name="keep", bufs=1))
        psum = ctx.enter_context(tc.psum_pool(name="psum", bufs=1))

        def sb(name, shape, dtype, tag=None):
            return keep.tile(shape, dtype, name=name, tag=tag or name, align_bytes=64)

        def load_list(name, src):
            t = sb(name, [P, PICKED // 16], U16)
            nc.sync.dma_start(t[:], src)
            return t

        def load_scales(table, src):
            for q in range(4):
                nc.sync.dma_start(table[32 * q : 32 * q + 4, :].bitcast(I32), src[0, 4 * q : 4 * q + 4, :].bitcast(I32))

        def load_words(name, src):
            t = sb(name, [P, TABLE], U32)
            nc.sync.dma_start(t[:].bitcast(I32), src[0].rearrange("p n t -> p (n t)").bitcast(I32))
            return t

        def load_weight(name, w):
            raw = sb(name + "_raw", [P, PACK, PACK * P], F32)
            nc.sync.dma_start(raw[:], w.rearrange("(p j) c -> p j c", j=PACK))
            return raw

        xs_tab = sb("xs_tab", [P, TABLE], U8)
        nc.gpsimd.memset(xs_tab[:].bitcast(I32), 0)
        es_tab = sb("es_tab", [P, TABLE], U8)
        nc.vector.memset(es_tab[:].bitcast(I32), 0)
        imm_tab = sb("imm_tab", [P, TABLE], F32)
        w1_raw = load_weight("w1", w1)
        offs_t = load_list("offs_t", offs)
        load_scales(xs_tab, x_scales)
        warm = sb("warm", [P, 1], F32)
        nc.gpsimd.memset(warm[:], 1.0)
        warm2 = sb("warm2", [P, 1], F32)
        nc.scalar.activation(warm2[:], warm[:], ACT.Ln)
        u1 = sb("u1", [P, PACK], F32)
        u2 = sb("u2", [P, PACK], F32)
        nc.gpsimd.dma_start(u2[:], unit2.rearrange("(p t) o -> p (t o)", t=PACK))
        nc.gpsimd.dma_start(u1[:], unit.rearrange("(p t) o -> p (t o)", t=PACK))
        xw_tab = load_words("xw_tab", x_words)
        agn_t = load_list("agn_t", agn)
        load_scales(es_tab, e_scales)
        w3_raw = load_weight("w3", w3)
        ew_tab = load_words("ew_tab", e_words)
        w2_raw = load_weight("w2", w2)
        mut_t = load_list("mut_t", mut)
        esc_t = load_list("esc_t", esc)
        nc.sync.dma_start(imm_tab[:], imm)

        def gather(name, table, offsets, dtype):
            t = sb(name, [P, PICKED], dtype)
            nc.vector.tensor_copy(t[:], table[:].indirect(offsets[:]))
            return t

        def gp_cast(dst, src):
            nc.gpsimd.tensor_scalar(dst, src, 1.0, 0.0, ALU.mult, ALU.add)

        def cast(copy, grouped, raw, m0, m1):
            dealt = grouped[:].rearrange("p (t m j) -> p m t j", t=PACK, j=PACK)
            copy(dealt[:, m0:m1], raw[:].rearrange("p j (m t) -> p m t j", t=PACK)[:, m0:m1])

        def quantise(grouped, codes, scales, calls):
            width = PACK * P // calls
            for c in range(calls):
                cols = slice(c * width, (c + 1) * width)
                nc.vector.quantize_mx(codes[:, cols].bitcast(FP8X4), scales[:, cols], grouped[:, c * width * PACK : (c + 1) * width * PACK])

        def product(tag, codes, scales, t, words, bytes_):
            bank = psum.tile([P, PICKED], F32, name=tag, tag=tag)
            cols = slice(t * P, (t + 1) * P)
            nc.tensor.matmul_mx(
                bank[:], lhsT=codes[:, cols].bitcast(FP8X4), lhsT_scale=scales[:, cols],
                rhs=words[:].bitcast(FP8X4), rhs_scale=bytes_[:], start=True, stop=True,
            )
            return bank

        def woven(tile):
            return tile[:].rearrange("p (c i t) -> p c t i", i=4, t=PACK)

        def planes(tile):
            return tile[:].rearrange("p t (c i) -> p c t i", i=4)

        w1_bf, w2_bf, w3_bf = [sb("w%d_bf" % w, [P, PACK * P * PACK], BF16) for w in (1, 2, 3)]
        w1_c, w2_c, w3_c = [sb("w%d_c" % w, [P, PACK * P], U32) for w in (1, 2, 3)]
        w1_s, w2_s, w3_s = [sb("w%d_s" % w, [P, PACK * P], U8) for w in (1, 2, 3)]
        logd = sb("logd", [P, PACK, PAIRS], F32)
        recip = sb("recip", [P, PACK, PAIRS], F32)
        immg = sb("immg", [P, PICKED], F32)
        hid = sb("hid", [P, PAIRS * PACK], BF16)
        hc = sb("hc", [P, PAIRS], U32)
        hs = sb("hs", [P, PAIRS], U8)
        z = [sb("z%d" % t, [P, PICKED], F32) for t in range(PACK)]
        yes = [sb("yes%d" % t, [P, PICKED], F32) for t in range(PACK)]
        ye = [None] * PACK
        epi = [sb("epi%d" % h, [P, PACK, HALF], F32) for h in range(2)]
        hid2 = [sb("hid2_%d" % h, [P, HALF * PACK], BF16) for h in range(2)]
        h2c = [sb("h2c%d" % h, [P, HALF], U32) for h in range(2)]
        h2s = [sb("h2s%d" % h, [P, HALF], U8) for h in range(2)]
        th = [sb("th%d" % b, [P, PICKED], F32) for b in range(2)]
        pre = [sb("pre%d" % b, [P, PICKED], F32) for b in range(2)]
        shifted = sb("shifted", [P, PICKED], F32)

        def paratope(t):
            y = product("a%d" % t, w1_c, w1_s, t, xw, xs)
            pair = y[:].rearrange("p (v d) -> p d v", d=2)
            absy = sb("absy%d" % t, [P, 2, PAIRS], F32)
            odd = sb("odd%d" % t, [P, PAIRS], F32)
            nc.scalar.activation(absy[:], pair, ACT.Abs)
            nc.scalar.activation(odd[:], pair[:, 1, :], ACT.Copy, scale=u1f[:, t : t + 1])
            nc.vector.tensor_tensor(big[:, t, :], absy[:, 0, :], absy[:, 1, :], ALU.max)
            nc.vector.scalar_tensor_tensor(su[:, t, :], pair[:, 0, :], u1f[:, t : t + 1], odd[:], ALU.mult, ALU.add)

        def rectify(t):
            yw = product("b%d" % t, w3_c, w3_s, t, ew, es)
            nc.scalar.activation(z[t][:], yw[:], ACT.Relu, scale=zsc[:, t : t + 1])

        def half(h):
            return slice(h * HALF, (h + 1) * HALF)

        def picks(lst, h):
            return lst[:, h * 16 : (h + 1) * 16]

        def fetch(t, h):
            nc.scalar.activation(yes[t][:, half(h)], z[t][:].indirect(picks(mut_t, h)), ACT.Copy)

        def join(t, h):
            nc.vector.scalar_tensor_tensor(epi[h][:, t, :], ye[t][:, half(h)], u2f[:, t : t + 1], yes[t][:, half(h)], ALU.mult, ALU.add)

        def fetch_join(t, h):
            nc.vector.tensor_tensor(epi[h][:, t, :], z[t][:].indirect(picks(mut_t, h)), yes[t][:, half(h)], ALU.add)

        def bind(h, b):
            tag = "b%d" % (2 * h + b)
            sc = psum.tile([P, HALF], F32, name=tag, tag=tag)
            rows = slice(b * P, (b + 1) * P)
            nc.tensor.matmul_mx(
                sc[:], lhsT=hc[:, rows].bitcast(FP8X4), lhsT_scale=hs[:, rows],
                rhs=h2c[h][:].bitcast(FP8X4), rhs_scale=h2s[h][:], start=True, stop=True,
            )
            nc.scalar.activation(th[b][:, half(h)], sc[:], ACT.Tanh)
            nc.vector.scalar_tensor_tensor(pre[b][:, half(h)], th[b][:, half(h)], 1.0, immg[:, half(h)], ALU.add, ALU.mult)

        def escape_fused(h):
            res = sb("res0_%d" % h, [P, HALF], F32)
            nc.vector.tensor_tensor(res[:], shifted[:].indirect(picks(esc_t, h)), pre[0][:, half(h)], ALU.mult)
            nc.sync.dma_start(out[0:P, half(h)], res[:])

        def escape_split(h):
            got = sb("got%d" % h, [P, HALF], F32)
            nc.scalar.activation(got[:], th[1][:].indirect(picks(esc_t, h)), ACT.Copy)
            res = sb("res1_%d" % h, [P, HALF], F32)
            nc.vector.scalar_tensor_tensor(res[:], got[:], -0.65 / 0.35, pre[1][:, half(h)], ALU.add, ALU.mult)
            nc.sync.dma_start(out[P : 2 * P, half(h)], res[:])

        cast(nc.scalar.copy, w1_bf, w1_raw, 0, 48)
        cast(nc.vector.tensor_copy, w1_bf, w1_raw, 48, 128)
        factors = sb("factors", [P, 4, PACK], F32, tag="w1_raw")
        flip, zsc, u2f, u1f = [factors[:, i, :] for i in range(4)]
        nc.scalar.activation(flip[:], u2[:], ACT.Sign, scale=-1.0)
        nc.scalar.activation(zsc[:], u2[:], ACT.Abs, scale=0.8)
        nc.scalar.activation(u2f[:], zsc[:], ACT.Copy, scale=-1.25)
        for t in range(PACK):
            nc.scalar.activation(u1f[:, t : t + 1], u1[:, t : t + 1], ACT.Copy, scale=flip[:, t : t + 1])
        quantise(w1_bf, w1_c, w1_s, 4)
        xs = gather("xs", xs_tab, offs_t, U8)
        xw = gather("xw", xw_tab, offs_t, U32)
        es = gather("es", es_tab, agn_t, U8)
        cast(nc.vector.tensor_copy, w3_bf, w3_raw, 0, 64)
        cast(nc.vector.tensor_copy, w3_bf, w3_raw, 64, 128)
        pooled = sb("pooled", [P, 2, PACK, PAIRS], F32, tag="w3_raw")
        big, su = pooled[:, 0], pooled[:, 1]
        paratope(0)
        paratope(1)
        paratope(2)
        paratope(3)
        quantise(w3_bf, w3_c, w3_s, 2)
        ew = gather("ew", ew_tab, agn_t, U32)
        nc.scalar.activation(logd[:, 0:2, :], big[:, 0:2, :], ACT.Ln, bias=0.5)
        nc.scalar.activation(logd[:, 2:4, :], big[:, 2:4, :], ACT.Ln, bias=0.5)
        rectify(0)
        rectify(1)
        rectify(2)
        rectify(3)
        cast(nc.vector.tensor_copy, w2_bf, w2_raw, 0, 64)
        cast(nc.vector.tensor_copy, w2_bf, w2_raw, 64, 128)
        quantise(w2_bf, w2_c, w2_s, 2)
        ye[0] = product("a0", w2_c, w2_s, 0, ew, es)
        nc.scalar.activation(yes[0][:], ye[0][:], ACT.Copy, scale=u2f[:, 0 : 1])
        ye[1] = product("a1", w2_c, w2_s, 1, ew, es)
        nc.scalar.activation(yes[1][:], ye[1][:], ACT.Copy, scale=u2f[:, 1 : 2])
        ye[2] = product("a2", w2_c, w2_s, 2, ew, es)
        ye[3] = product("a3", w2_c, w2_s, 3, ew, es)
        fetch(2, 0)
        fetch(3, 0)
        fetch(2, 1)
        fetch(3, 1)
        nc.scalar.activation(recip[:], logd[:], ACT.Exp, scale=-1.0)
        nc.scalar.activation(immg[:], imm_tab[:].indirect(agn_t[:]), ACT.Copy, scale=-0.175)
        nc.vector.tensor_tensor(woven(hid), planes(su), planes(recip), ALU.mult)
        nc.vector.quantize_mx(hc[:].bitcast(FP8X4), hs[:], hid[:])
        fetch_join(0, 0)
        fetch_join(1, 0)
        join(2, 0)
        join(3, 0)
        nc.scalar.copy(woven(hid2[0]), planes(epi[0]))
        nc.vector.quantize_mx(h2c[0][:].bitcast(FP8X4), h2s[0][:], hid2[0][:])
        fetch_join(0, 1)
        fetch_join(1, 1)
        join(2, 1)
        join(3, 1)
        nc.vector.tensor_copy(woven(hid2[1]), planes(epi[1]))
        nc.vector.quantize_mx(h2c[1][:].bitcast(FP8X4), h2s[1][:], hid2[1][:])
        bind(0, 0)
        bind(1, 0)
        nc.scalar.activation(shifted[:], th[0][:], ACT.Copy, bias=-0.65 / 0.35)
        bind(0, 1)
        bind(1, 1)
        escape_fused(0)
        escape_fused(1)
        escape_split(0)
        escape_split(1)
